import numpy as np, ml_dtypes
CORES = [1,5,17,21,33,37,49,53]
N = 8
BF = ml_dtypes.bfloat16
def gentries(a):
    return np.ascontiguousarray(a.reshape(8, 16, -1).transpose(0, 2, 1)).reshape(8, -1)
def gtable(e):
    e = np.asarray(e); return np.ascontiguousarray(e.reshape(8, -1, 16).transpose(0, 2, 1)).reshape(128, -1).astype(np.int32)
C, M, G, T, TH, S = 4096, 1024, 512, 3, 9, 8
def parts(rng):
    R = rng.integers(0, 256, (N, 8, 16, C)); P = rng.integers(0, M, (N, 8, 16, M)); O = rng.integers(0, M, (N, 8, 16, M))
    z = (256 * rng.choice(np.array([0.6, 0.8, 1.0]), (N, 8, 1, G)) * rng.random((N, 8, 16, G))).astype(np.int64)
    return R, P, O, z, rng.integers(0, M, (N, 8, G)), rng.integers(1, 257, (N, 8, 16))
def pack(R, P, O, z, mv, w):
    P = np.array(P); O = np.array(O); P[:, :, 0] = np.arange(M); O[:, :, 0] = np.arange(M)
    return {"strat": R.reshape(N, 128, C).astype(np.float32).astype(BF), "vp": P.reshape(N, 128, M).astype(np.int32), "vo": O.reshape(N, 128, M).astype(np.int32),
            "z0": z.reshape(N, 128, G).astype(np.float32).astype(BF), "mv": np.stack([gtable(a) for a in mv]), "wt": w.reshape(N, 128, 1).astype(np.int32)}
def plant(rng, R, P, O, z, mv, w):
    h = 17 - TH; m = np.arange(M)
    w[:, :, 13] = 16; w[:, :, 14] = 1; w[:, 2, :13] = np.maximum(w[:, 2, :13], 160)
    for r in range(N):
        q = (r + 1) % N
        for g in range(8):
            own = rng.permutation(M)[:12]; i = 1 + rng.permutation(G - 17)[:5]; wq = w[q, g]
            for e in range(4):
                a = int(i[e]); mv[r, g, a] = own[e]; P[r, g, 3 + 4 * e, own[e]] = M - 1
                z[r, g, :h, a] = 255; z[r, g, 13:15, a] = 0
                d = (4065 - int(np.sum(wq * z[r, g, :, a]))) & 4095
                z[r, g, 13, a] = d >> 4; z[r, g, 14, a] = d & 15
            if g == 2:
                left = 2 ** 19
                for j in list(range(13)) + [15, 13, 14]:
                    n = min(255, left // int(wq[j])); z[r, g, j, int(i[4])] = n; left -= n * int(wq[j])
            end = G - 15 + 2 * np.arange(8); mv[r, g, end] = own[4:]
            z[r, g, :h, G - 15::2] = 255
            u = np.sum(wq[:, None] * z[r, g], axis=0) & 4095; p0 = int(u[0]) & (S - 1)
            R[q, g, :, p0] = 255 * rng.integers(0, 2, 16)
            ad = (((m[:, None] * u[end][None, :]) >> 5) + m[:, None] + 37 * 15) & (C - 1)
            for e in range(8):
                good = np.flatnonzero(ad[:, e] == p0)
                if len(good): P[r, g, 15, own[4 + e]] = rng.choice(good)
    return R, P, O, z, mv, w
def setup_inputs(rng):
    return pack(*plant(rng, *parts(rng)))
def corner(rng, first):
    R, P, O, z, mv, w = parts(rng); R = np.maximum(R, 1); m = np.arange(M)[None, :]; j = np.arange(16)[:, None]
    forms = [m + 0 * j, np.maximum(m - j, 0), np.minimum(m + j, M - 1), np.where((m + j) % 2 == 0, 0, M - 1)]
    P = np.stack([np.stack([forms[(g + r) % 4] for g in range(8)]) for r in range(N)])
    O = np.stack([np.stack([forms[(g + r + 1 + g // 4) % 4] for g in range(8)]) for r in range(N)])
    cnt = np.array([255, 256, 1024, 512, 257, 511, 1, 8 * G - 1, 8 * G, 0, 1536, 4 * G, 6 * G, 8 * G - 256, 1023, 1025])[first * N:first * N + N]
    cnt = np.roll(cnt, int(rng.integers(0, N)))
    for r in range(N):
        for g in range(8):
            e = (g + r) % 3
            if e == 0: mv[r, g] = rng.choice(np.array([0, M - 1]), G)
            elif e == 1: mv[r, g] = rng.integers(0, M)
            else: mv[r, g] = rng.permutation(M)[:G]
        hit = np.zeros(8 * G, bool); hit[rng.permutation(8 * G)[:int(cnt[r])]] = True
        z[r] = np.where(hit.reshape(8, 1, G), 0, 255)
    w[:, 1] = 1; w[:, 5] = 256
    return pack(R, P, O, z, mv, w)
def setup_inputs_corners(rng):
    return corner(rng, 0)
def setup_inputs_corners_two(rng):
    return corner(rng, 1)
def setup_inputs_ends(rng):
    R = np.where(rng.random((N, 8, 16, C)) < rng.choice(np.array([0.1, 0.5, 0.75, 0.9]), (N, 8, 1, C)), 255, 0)
    z = np.where(rng.random((N, 8, 16, G)) < rng.choice(np.array([0.05, 0.3, 0.8]), (N, 8, 1, G)), 255, 0)
    P = (M - 1) * rng.integers(0, 2, (N, 8, 16, M)); O = (M - 1) * rng.integers(0, 2, (N, 8, 16, M)); mv = (M - 1) * rng.integers(0, 2, (N, 8, G))
    w = np.where(rng.random((N, 8, 16)) < 0.5, 256, 1)
    mv[:, :, G - 1] = M - 1; P[:, :, 15, M - 1] = M - 1; O[:, :, 15, M - 1] = M - 1
    w[:, 0] = 256; R[:, 0] = np.where(rng.random((N, 1, C)) < 0.5, 255, 0); z[:, 0, :, G - 1] = 255; z[:, 0, :, 0] = 0
    w[:, 5:] = 256; w[:, 5:, 15] = 1
    c = np.zeros(16, np.int64); c[3] = 255; c[15] = 255
    x8 = np.array([0, 1, 2, 4, 5, 6, 7, 8]); y4 = np.array([9, 10, 11, 12])
    for g in (6, 7):
        hot = ((np.arange(C) >> 7) + g) % 2 == 1
        R[:, g] = c[None, :, None]
        R[:, g, x8] = np.where(hot, 192, 64 * rng.integers(0, 2, (N, 1, C))); R[:, g, y4] = np.where(hot, 128, 0)
        z[:, g, :, 1::2] = c[None, :, None]; z[:, g, :, G - 1] = c[None, :]
    R[:, 5] = 0; R[:, 5, 15] = 255; R[:, 5, y4] = 128 * rng.integers(0, 2, (N, 1, C))
    R[:, 5, x8, C - 1] = 192; R[:, 5, y4, C - 1] = 128
    z[:, 5] = 0; z[:, 5, 15] = 255
    m = np.arange(M); f = ((m * 255) >> 5) + m
    for j in range(1, 14):
        near = m[((f + 37 * (j + 1)) & (C - 1)) >= C - 256]
        P[:, 5, j] = rng.choice(near, (N, M)); O[:, 5, j] = rng.choice(near, (N, M))
    P[:, 5, 14:] = rng.integers(0, M, (N, 2, M)); O[:, 5, 14:] = rng.integers(0, M, (N, 2, M))
    mv[:, 5] = np.argsort(rng.random((N, M)), axis=1)[:, :G]; mv[:, 5, G - 1] = M - 1
    keep = np.array(R[3, 5])
    z[1, :, :17 - TH] = 255; z[2, :, :TH] = 0; R[3, :, :TH] = 255
    a0 = f[mv[2, 5]] & (C - 1); keep[np.ix_(x8, a0)] = 192; keep[np.ix_(y4, a0)] = 128; R[3, 5] = keep
    return pack(R, P, O, z, mv, w)
def setup_inputs_spread(rng):
    R = np.minimum((np.exp2(8 * rng.random((N, 8, 1, C))) * rng.random((N, 8, 16, C))).astype(np.int64), 255)
    z = np.minimum((np.exp2(8 * rng.random((N, 8, 1, G))) * rng.random((N, 8, 16, G))).astype(np.int64), 255)
    P = np.minimum((M * rng.random((N, 8, 16, M)) ** 3).astype(np.int64), M - 1); O = np.minimum((M * rng.random((N, 8, 16, M)) ** 3).astype(np.int64), M - 1)
    mv = np.minimum((M * rng.random((N, 8, G)) ** 2).astype(np.int64), M - 1)
    w = np.minimum(np.maximum(np.rint(np.exp2(8 * rng.random((N, 8, 16)))).astype(np.int64), 1), 256)
    v0 = [v for v in range(M + G * (T - 2), M + G * (T - 1)) if (-(2 ** 22)) % v < 32][0]
    u0 = (2 ** 22 + v0 - 1) // v0 - 32
    r = int(rng.integers(0, N)); q = (r + 1 + (T - 1) % (N - 1)) % N; p = (r + 1 + (T - 2) % (N - 1)) % N
    R[q, :, :17 - TH] = 0
    for g in (1, 3, 4, 6):
        w[q, g, 13] = 16; w[q, g, 14] = 1
        c = rng.integers(0, 256, 16); c[13:15] = 0
        d = (u0 - int(np.sum(w[q, g] * c))) & 4095
        c[13] = d >> 4; c[14] = d & 15
        R[p, g] = c[:, None]
        R[q, g, 15] = 0; R[q, g, 15, 0] = 255
    return pack(R, P, O, z, mv, w)
def setup_inputs_ties(rng):
    R, P, O, z, mv, w = parts(rng)
    b = rng.integers(0, 255, (8, 16)); b[0] = 0; b[6] = 254
    share = rng.permutation(np.array([0.02, 0.04, 0.07, 0.1, 0.15, 0.2, 0.3, 0.5])).reshape(1, 8, 1, 1)
    cnt = np.where(rng.random((N, 8, 1, C)) < share, rng.choice(np.array([TH, TH, TH, TH + 1, 16]), (N, 8, 1, C)), rng.choice(np.array([TH - 1, TH - 1, TH - 1, 0]), (N, 8, 1, C)))
    R = b[None, :, :, None] + (np.argsort(rng.random((N, 8, 16, C)), axis=2) < cnt)
    z = b[None, :, :, None] + (rng.random((N, 8, 1, G)) < 0.125) + np.zeros((N, 8, 16, G), np.int64)
    return pack(R, P, O, z, mv, w)
def check_inputs(d):
    bad = []
    for k, lo, hi in (("strat", 0, 255), ("vp", 0, M - 1), ("vo", 0, M - 1), ("z0", 0, 255), ("mv", 0, M - 1), ("wt", 1, 256)):
        a = np.asarray(d[k]).astype(np.float64)
        if not (np.min(a) >= lo and np.max(a) <= hi): bad.append("range of " + k)
        elif np.any(a != np.floor(a)): bad.append("whole numbers in " + k)
    for k in ("vp", "vo"):
        if np.any(np.asarray(d[k]).reshape(-1, 8, 16, M)[:, :, 0] != np.arange(M)): bad.append("row 0 of the views in " + k)
    return bad
def reference(strat, vp, vo, z0, mv, wt):
    R = strat.astype(np.float32).astype(np.int32).reshape(N, 8, 16, C); z = z0.astype(np.float32).astype(np.int32).reshape(N, 8, 16, G)
    w = wt.astype(np.int32).reshape(N, 8, 16, 1); v = np.stack([gentries(a) for a in mv]).astype(np.int64)
    room = np.zeros((N, 8, 16, G * T), np.int32)
    views = [np.concatenate([a.astype(np.int32).reshape(N, 8, 16, M), room], axis=3) for a in (vp, vo)]
    count = np.zeros(N, np.int64); kk = np.arange(16)[None, None, :, None]; verdicts = np.zeros((N, 8, T, G), np.int64)
    for t in range(T):
        mover, other = views[t % 2], views[1 - t % 2]
        q = (np.arange(N) + 1 + t % (N - 1)) % N
        L = np.take_along_axis(mover, v[:, :, None, :], 3).astype(np.int64)
        u = np.add.reduce(w[q] * z, axis=2).astype(np.int64) & 4095
        ad = (((L * u[:, :, None, :]) >> 5) + L + 37 * kk + (count[q] & 255)[:, None, None, None]) & (C - 1)
        Y = np.take_along_axis(R[q], ad.reshape(N, 8, 1, 16 * G), 3).reshape(N, 8, 16, 16, G)
        hit = np.add.reduce((Y > z[:, :, :, None, :]).astype(np.int32), axis=2) >= TH
        hit[:, :, 15] = True
        kap = np.argmax(hit, axis=2)
        use = (kk <= kap[:, :, None, :])[:, :, None]
        z = (np.maximum.reduce(np.where(use, Y, 0), axis=3) + np.minimum.reduce(np.where(use, Y, 255), axis=3)) >> 1
        z = z.astype(np.int32)
        if t < T - 1:
            place = S * np.arange(G) + (u & (S - 1))
            for r in range(N):
                ix = np.repeat(place[r][:, None, :], 16, axis=1); mine = R[int(q[r])]
                np.put_along_axis(mine, ix, (np.take_along_axis(mine, ix, 2) + z[r]) >> 1, 2)
        count[q] = np.add.reduce((kap < 15).reshape(N, 8 * G).astype(np.int64), axis=1)
        named = np.take_along_axis(L, kap[:, :, None, :], 2)
        resumed = np.take_along_axis(other, named, 3)
        n0 = M + G * t; n = np.zeros((N, 8, 1, G), np.int64) + n0 + np.arange(G)
        mover[..., n0:n0 + G] = np.concatenate([n, L[:, :, :15]], axis=2)
        other[..., n0:n0 + G] = np.concatenate([n, resumed[:, :, :15]], axis=2)
        v = n[:, :, 0]; verdicts[:, :, t] = kap
    e = M + G * (T - 1)
    return {"yp": views[0][..., e:e + G].reshape(N, 128, G).astype(np.float32), "yo": views[1][..., e:e + G].reshape(N, 128, G).astype(np.float32),
            "yz": z.reshape(N, 128, G).astype(np.float32).astype(BF), "yk": verdicts.reshape(N, 8, T * G).astype(np.float32)}

@@ -1,0 +1,562 @@
+from concourse.mybir import AluOpType as ALU, AxisListType, ActivationFunctionType as ACTF
+
+NT, G, NC, CH = 3, 512, 4, 128
+RW = 4096 + 816
+QA = (3,)
+DG = (2, 3)
+EN = 8
+
+SCRATCH = {
+    "rw": ("sbuf", [128, RW], "bfloat16"), "pt": ("sbuf", [128, 1536], "int32"), "ot": ("sbuf", [128, 2048], "int32"),
+    "mvs": ("sbuf", [128, 32], "int32"), "mvu": ("sbuf", [128, 32], "uint16"),
+    "wti": ("sbuf", [128, 8], "int32"), "zst": ("sbuf", [128, G], "bfloat16"),
+    "yy": ("sbuf", [128, 16 * G], "bfloat16"), "hi": ("sbuf", [128, 16 * G], "bfloat16"), "lo": ("sbuf", [128, 16 * G], "bfloat16"),
+    "bt": ("sbuf", [128, 16 * G], "bfloat16"), "mhi": ("sbuf", [128, 16 * CH], "bfloat16"), "mlo": ("sbuf", [128, 16 * CH], "bfloat16"),
+    "qf": ("sbuf", [128, G], "float16"), "xi": ("sbuf", [128, G], "int32"), "ai": ("sbuf", [128, G], "int32"),
+    "hit": ("sbuf", [128, G], "bfloat16"), "oh": ("sbuf", [128, 2 * G], "float16"),
+    "hp": ("sbuf", [128, G], "bfloat16"), "sm": ("sbuf", [128, G], "float16"), "z16": ("sbuf", [128, G], "float16"),
+    "old": ("sbuf", [128, G], "bfloat16"), "nw": ("sbuf", [128, G], "int32"), "res": ("sbuf", [128, G], "float16"),
+    "pli": ("sbuf", [128, 32], "int32"), "plm": ("sbuf", [128, 32], "int32"), "plu": ("sbuf", [128, 32], "uint16"),
+    "kint": ("sbuf", [128, 32], "int32"), "kand": ("sbuf", [128, 32], "int32"), "kf": ("sbuf", [128, 32], "bfloat16"),
+    "yps": ("sbuf", [128, G], "float32"), "yos": ("sbuf", [128, G], "float32"), "yks": ("sbuf", [128, NT * G], "float32"),
+    "acc": ("sbuf", [128, 4 * NT], "float32"), "an": ("sbuf", [128, 4], "float32"), "ani": ("sbuf", [128, 8], "int32"),
+    "xint": ("sbuf", [128, G], "int32"), "xgi": ("sbuf", [128, 128], "int32"), "xx": ("sbuf", [128, G], "float32"), "xg": ("sbuf", [128, 128], "float32"),
+    "pint": ("sbuf", [128, 8], "int32"), "col": ("sbuf", [128, 32], "float32"),
+    "zb_": ("sbuf", [128, 144], "bfloat16"), "zh_": ("sbuf", [128, 144], "float16"), "zw_": ("sbuf", [128, 144], "bfloat16"),
+    "bw": ("sbuf", [128, 128], "bfloat16"), "bb": ("sbuf", [128, 128], "bfloat16"), "ib": ("sbuf", [128, 128], "bfloat16"),
+    "nib": ("sbuf", [128, 128], "bfloat16"), "hib": ("sbuf", [128, 128], "bfloat16"), "ih": ("sbuf", [128, 128], "float16"),
+    "i4": ("sbuf", [128, 128], "float16"), "sh": ("sbuf", [128, 128], "float16"), "tri": ("sbuf", [128, 128], "bfloat16"), "tr2": ("sbuf", [128, 128], "bfloat16"),
+    "kc": ("sbuf", [128, 128], "float16"), "one": ("sbuf", [128, G], "float16"), "it2": ("sbuf", [128, G], "float16"),
+    "a15": ("sbuf", [128, 128], "float32"), "cst": ("sbuf", [128, 16], "float16"), "c8": ("sbuf", [128, 32], "int32"),
+}
+for _t in range(NT):
+    SCRATCH["nn%d" % _t] = ("sbuf", [128, 128], "float16")
+    SCRATCH["li%d" % _t] = ("sbuf", [128, G], "float16")
+    SCRATCH["ls%d" % _t] = ("sbuf", [128, G], "float16")
+    SCRATCH["of%d" % _t] = ("sbuf", [128, G], "uint16")
+    SCRATCH["sb%d" % _t] = ("sbuf", [128, 16 * NC], "uint16")
+    SCRATCH["nm%d" % _t] = ("sbuf", [128, 16 * NC], "uint16")
+    SCRATCH["zo%d" % _t] = ("sbuf", [128, G], "bfloat16")
+for _t in range(NT + 1):
+    SCRATCH["zi%d" % _t] = ("sbuf", [128, G], "bfloat16")
+BANKS = ("pz", "pd0", "pd1", "pc", "pf", "pr", "pu", "ps")
+for _b in BANKS:
+    SCRATCH[_b] = ("psum", [128, 512], "float32")
+
+LDS = ["ld_mv", "ld_wt", "ld_z", "ld_p", "ld_o", "ld_r"]
+OUTS = ["o_p", "o_o0", "o_o1", "o_z0", "o_z1", "o_k0", "o_k1", "o_k2"]
+SEMAPHORES = ["qv", "qs", "qp", "qg", "loc", "za0", "la0", "lb0"] + LDS + OUTS
+for _t in range(NT):
+    for _c in range(NC):
+        SEMAPHORES += ["nm%d%d" % (_t, _c), "za%d%d" % (_t + 1, _c)]
+        if _t:
+            SEMAPHORES.append("la%d%d" % (_t, _c))
+
+
+def rank_program(g, core, T, topo):
+    me = T.rank_of(core)
+    if me is None:
+        return
+    cores = list(T.cores)
+    N = len(cores)
+    Q = {"v": g.vector, "s": g.scalar, "p": g.tensor, "g": g, "y": g.sync}
+    cnt, known, recs = {}, {e: {} for e in Q}, {}
+
+    def need(e, tok):
+        sem, val, vc = tok
+        k = known[e]
+        if k.get(sem, 0) >= val:
+            return
+        Q[e].wait_ge(T.sem[sem], val)
+        k[sem] = val
+        for s2, v2 in vc.items():
+            if k.get(s2, 0) < v2:
+                k[s2] = v2
+
+    def deps(e, eng, reads, writes):
+        for w, lst in ((0, reads), (1, writes)):
+            for n, lo, hi in lst:
+                for rec in recs.get(n, ()):
+                    if n in BANKS:
+                        hit = rec[3] != eng or (eng != "p" and (w or rec[2]))
+                    else:
+                        hit = rec[0] < hi and lo < rec[1] and (rec[2] or (w and rec[3] != eng))
+                    if hit:
+                        need(e, rec[4])
+
+    def note(eng, tok, reads, writes):
+        for w, lst in ((0, reads), (1, writes)):
+            for n, lo, hi in lst:
+                old = recs.get(n, [])
+                if n in BANKS:
+                    w0 = any(r[2] for r in old if r[3] == eng)
+                    recs[n] = [(lo, hi, w or w0, eng, tok)]
+                    continue
+                if w:
+                    old = [r for r in old if not (lo <= r[0] and r[1] <= hi)]
+                else:
+                    old = [r for r in old if not (r[3] == eng and not r[2] and lo <= r[0] and r[1] <= hi)]
+                recs[n] = old + [(lo, hi, w, eng, tok)]
+
+    def A(n, lo=0, hi=None, st=1, p=128):
+        t = T[n]
+        hi = t.shape[1] if hi is None else hi
+        return (t[0:p, lo:hi:st], (n, lo, hi)) if st > 1 else (t[0:p, lo:hi], (n, lo, hi))
+
+    def run(e, fn, reads, writes, inc=True):
+        rd, wr = [r[1] for r in reads], [w[1] for w in writes]
+        deps(e, e, rd, wr)
+        ins = fn(Q[e])
+        sem = "q" + e
+        val = cnt.get(sem, 0) + 1
+        if inc:
+            ins.then_inc(T.sem[sem], 1)
+            cnt[sem] = val
+        note(e, (sem, val, dict(known[e])), rd, wr)
+
+    def dma(e, sem, out, in_, reads=(), writes=()):
+        rd, wr = [r[1] for r in reads], [w[1] for w in writes]
+        deps(e, "d" + sem, rd, wr)
+        Q[e].dma_start(out, in_).then_inc(T.sem[sem], 16)
+        cnt[sem] = cnt.get(sem, 0) + 16
+        note("d" + sem, (sem, cnt[sem], dict(known[e])), rd, wr)
+
+    def arrives(buf, lo, hi, sem):
+        recs.setdefault(buf, []).append((lo, hi, 1, "r", (sem, EN, {})))
+
+    def send(buf, src, lo, hi, sem, to):
+        dst = cores[to % N]
+        deps("g", "r", [(src, lo, hi)], [])
+        rid, pid, _ = topo.addr(dst)
+        m = 0
+        for x in topo.engines(core, dst)[:EN]:
+            m |= 1 << x
+        g.remote_dma(T[buf][:, lo:hi], T[src][:, lo:hi], T.sem[sem], T.sem["loc"], pid, rid, m)
+        cnt["loc"] = cnt.get("loc", 0) + EN
+
+    def mm(out, l, r, start=True, stop=True, inc=None):
+        run("p", lambda q: q.matmul(out[0], l[0], r[0], start, stop), [l, r], [out], stop if inc is None else inc)
+
+    def copy(out, in_):
+        run("v", lambda q: q.tensor_copy(out[0], in_[0]), [in_], [out])
+
+    def ts(out, in_, s1, op0, s2=None, op1=None):
+        rd = [in_] + [s for s in (s1, s2) if isinstance(s, tuple)]
+        a1 = s1[0] if isinstance(s1, tuple) else s1
+        a2 = s2[0] if isinstance(s2, tuple) else s2
+        if op1 is None:
+            run("v", lambda q: q.tensor_scalar(out[0], in_[0], a1, None, op0), rd, [out])
+        else:
+            run("v", lambda q: q.tensor_scalar(out[0], in_[0], a1, a2, op0, op1), rd, [out])
+
+    def tt(out, a, b, op):
+        run("v", lambda q: q.tensor_tensor(out[0], a[0], b[0], op), [a, b], [out])
+
+    def act(out, in_, fn, acc=None, **kw):
+        if acc is None:
+            run("s", lambda q: q.activation(out[0], in_[0], fn, **kw), [in_], [out])
+        else:
+            run("s", lambda q: q.activation(out[0], in_[0], fn, accum_out=acc[0], **kw), [in_], [out, acc])
+
+    def gather_v(out, win, off):
+        run("v", lambda q: q.tensor_copy(out[0], win[0].indirect(off[0])), [win, off], [out])
+
+    def gather_s(out, win, off):
+        run("s", lambda q: q.activation(out[0], win[0].indirect(off[0]), ACTF.Copy), [win, off], [out])
+
+    def fill(out, c):
+        run("v", lambda q: q.memset(out[0], c), [], [out])
+
+    def iota(out, pattern, base, cm):
+        run("g", lambda q: q.iota(out[0], pattern, base, cm), [], [out])
+
+    arrives("zi0", 0, G, "za0")
+    arrives("li0", 0, CH, "la0")
+    arrives("li0", CH, G, "lb0")
+    for t in range(NT):
+        for c in range(NC):
+            arrives("nm%d" % t, 16 * c, 16 * c + 16, "nm%d%d" % (t, c))
+            arrives("zi%d" % (t + 1), CH * c, CH * c + CH, "za%d%d" % (t + 1, c))
+            if t:
+                arrives("li%d" % t, CH * c, CH * c + CH, "la%d%d" % (t, c))
+
+    dma("s", "ld_z", T.zst[:], T.z0[:], writes=[A("zst")])
+    dma("y", "ld_mv", T.mvs[:], T.mv[:], writes=[A("mvs")])
+    dma("y", "ld_p", T.pt[:, 0:1024], T.vp[:], writes=[A("pt", 0, 1024)])
+    dma("s", "ld_wt", T.wti[:, 0:1], T.wt[:], writes=[A("wti", 0, 1)])
+    dma("s", "ld_r", T.rw[:, 0:4096], T.strat[:], writes=[A("rw", 0, 4096)])
+    dma("y", "ld_o", T.ot[:, 0:1024], T.vo[:], writes=[A("ot", 0, 1024)])
+
+    C = lambda i: A("col", i, i + 1)
+    cp, ck, cg16, cz15, c37, ck16, c8k, cj0, cj1, cnl, cshp, cthr, cw, cg, ct, cadd = [C(i) for i in range(16)]
+    cv = [C(16 + i) for i in range(NT)]
+
+    def addr1(t, lo, hi):
+        mm(A("pu", 0, hi - lo), A("bw"), A("zi%d" % t, lo, hi))
+
+    def addr2(t, lo, hi):
+        n = hi - lo
+        pu = A("pu", 0, n)
+        ts(A("qf", lo, hi), pu, 1.0 / 4096, ALU.mult, 1025 - 2047.5 / 4096, ALU.add)
+        mm(pu, A("kc"), A("one", 0, n), True, False)
+        mm(pu, A("bw"), A("zi%d" % t, lo, hi), False, False)
+        mm(pu, A("i4"), A("qf", lo, hi), False, True)
+
+    def addr3(t, lo, hi):
+        tt(A("xi", lo, hi), A("li%d" % t, lo, hi), A("pu", 0, hi - lo), ALU.mult)
+        ts(A("ai", lo, hi), A("xi", lo, hi), 5, ALU.arith_shift_right, 4095, ALU.bitwise_and)
+
+    def addr(t, lo, hi):
+        addr1(t, lo, hi)
+        addr2(t, lo, hi)
+        addr3(t, lo, hi)
+
+    def afin(t, lo, hi):
+        ts(A("of%d" % t, lo, hi), A("ai", lo, hi), cadd if t else c37, ALU.add)
+
+    def gath(t, c, pieces, e="s"):
+        for s in pieces:
+            i0 = CH * c + 32 * s
+            (gather_s if e == "s" else gather_v)(A("yy", 16 * i0, 16 * i0 + 512), A("rw", 0, RW), A("of%d" % t, i0, i0 + 32))
+
+    def blk(c, q):
+        return (2048 * c + 512 * q, 2048 * c + 512 * q + 512)
+
+    def zx(t, c):
+        for e in range(4):
+            mm(A("pz", e, 512, 4), A("ib"), A("zi%d" % t, CH * c, CH * c + CH), inc=e == 3)
+
+    def cmpv(t, c):
+        for q in range(4):
+            if q not in QA:
+                tt(A("bt", *blk(c, q)), A("yy", 2048 * c + q, 2048 * c + 2048, 4), A("pz"), ALU.is_gt)
+
+    def bank(c, q):
+        return "pd%d" % ((c * len(QA) + QA.index(q)) % 2)
+
+    def diff(t, c):
+        for q in QA:
+            mm(A(bank(c, q)), A("ib"), A("yy", 2048 * c + q, 2048 * c + 2048, 4), True, False)
+            for e in range(4):
+                mm(A(bank(c, q), e, 512, 4), A("nib"), A("zi%d" % t, CH * c, CH * c + CH), False, e == 3)
+
+    def cmps(t, c):
+        for q in QA:
+            act(A("bt", *blk(c, q)), A(bank(c, q)), ACTF.Sign, bias=-0.5)
+
+    def count(t, c):
+        ks = [(q, m) for q in [q for q in range(4) if q not in QA] + list(QA) for m in range(4)]
+        for n, (q, m) in enumerate(ks):
+            k = 4 * m + q
+            lo, hi = blk(c, q)
+            mm(A("pc", 0, CH), A("zb_", 15 - k, 143 - k), A("bt", lo + m, hi, 4), n == 0, n == 15)
+
+    def scan(t, c, hi):
+        s = (2048 * c, 2048 * c + 2048)
+        o, m = (A("hi", *s), A("mhi")) if hi else (A("lo", *s), A("mlo"))
+        o0, o1 = (ALU.min, ALU.max) if hi else (ALU.max, ALU.min)
+        y = A("yy", *s)
+        run("v", lambda q: q.tensor_tensor_scan(o[0], m[0], y[0], 0.0, o0, o1), [m, y], [o])
+
+    def hits(t, c):
+        h = A("hit", CH * c, CH * c + CH)
+        ts(h, A("pc", 0, CH), cthr, ALU.is_ge)
+        mm(A("pf", 0, CH), A("tri"), h)
+
+    def lists1(t, c):
+        o = 2 * CH * c
+        act(A("pr", 0, CH), A("pf", 0, CH), ACTF.Relu, acc=A("acc", 4 * t + c, 4 * t + c + 1), scale=4096.0)
+        ts(A("oh", o, o + CH), A("pf", 0, CH), 0.0, ALU.max, ck, ALU.mult)
+        tt(A("oh", o + CH, o + 2 * CH), A("li%d" % t, CH * c, CH * c + CH), A("pr", 0, CH), ALU.min)
+        pl = A("pf", 256, 272)
+        mm(pl, A("ih"), A("cst"), True, False)
+        for k in range(16):
+            mm(pl, A("zh_", 15 - k, 143 - k), A("oh", o + k, o + 2 * CH, 16), False, k == 15)
+
+    def lists2(t, c):
+        copy(A("sb%d" % t, 16 * c, 16 * c + 16), A("pf", 256, 272))
+        send("nm%d" % t, "sb%d" % t, 16 * c, 16 * c + 16, "nm%d%d" % (t, c), me - 1 - t)
+
+    def pick1(t, c):
+        a, b = CH * c, CH * c + CH
+        gather_s(A("hp", a, b), A("hi", 16 * a, 16 * b), A("sb%d" % t, 16 * c, 16 * c + 8))
+
+    def pick2(t, c):
+        a, b = CH * c, CH * c + CH
+        off, w, h, s = A("sb%d" % t, 16 * c, 16 * c + 8), A("lo", 16 * a, 16 * b), A("hp", a, b), A("sm", a, b)
+        run("v", lambda q: q.tensor_tensor(s[0], w[0].indirect(off[0]), h[0], ALU.add), [w, off, h], [s])
+        ts(A("z16", a, b), s, 0.5, ALU.mult, 1024.75, ALU.add)
+        ts(A("zo%d" % t, a, b), A("z16", a, b), -1025.0, ALU.add)
+        send("zi%d" % (t + 1), "zo%d" % t, a, b, "za%d%d" % (t + 1, c), me + 1 if t + 1 < NT else me - 1 - t)
+
+    def place1(t):
+        for k in range(16):
+            mm(A("pr", 256, 288), A("zw_", 15 - k, 143 - k), A("zi%d" % t, k, G, 16), k == 0, k == 15)
+
+    def place2(t):
+        copy(A("pli"), A("pr", 256, 288))
+        ts(A("plm"), A("pli"), 7, ALU.bitwise_and)
+        tt(A("pli"), A("plm"), A("c8"), ALU.add)
+        copy(A("plu"), A("pli"))
+
+    def olds(t):
+        gather_s(A("old"), A("rw", 0, 4096), A("plu"))
+
+    def upd1(t, lo, hi):
+        mm(A("ps", CH, CH + hi - lo), A("hib"), A("old", lo, hi), True, False)
+        mm(A("ps", CH, CH + hi - lo), A("hib"), A("zo%d" % t, lo, hi), False, True)
+
+    def upd2(t, lo, hi):
+        ts(A("nw", lo, hi), A("ps", CH, CH + hi - lo), -0.25, ALU.add)
+
+    def scat(t, lo, hi):
+        w, o, i = A("rw", 0, 4096), A("plu", lo // 16, hi // 16), A("nw", lo, hi)
+        run("v", lambda q: q.tensor_copy(w[0].indirect(o[0]), i[0]), [o, i], [w])
+
+    def mirror(t):
+        copy(A("rw", 4096, RW), A("rw", 0, RW - 4096))
+
+    def tally1(t):
+        mm(A("pr", 320, 324), A("a15"), A("acc", 4 * t, 4 * t + 4))
+
+    def tally2(t):
+        o, i = A("an", 0, 1), A("pr", 320, 324)
+        run("v", lambda q: q.tensor_reduce(o[0], i[0], AxisListType.X, ALU.add, negate=True), [i], [o])
+        copy(A("ani", 0, 1), o)
+        ts(A("ani", 1, 2), A("ani", 0, 1), 255, ALU.bitwise_and)
+        ts(cadd, A("ani", 1, 2), c37, ALU.add)
+
+    def shift(t, src, lo, hi, b="ps"):
+        p = A(b, 0, hi - lo)
+        mm(p, A("sh"), A(src, lo, hi), True, False)
+        mm(p, A("nn%d" % t), A("it2", lo, hi), False, True)
+
+    def home1(t, c):
+        a, b = CH * c, CH * c + CH
+        gather_v(A("res", a, b), A(("ot", "pt", "ot")[t], 0, 1024 + 512 * t), A("nm%d" % t, 16 * c + 8, 16 * c + 16))
+        shift(t, "res", a, b)
+
+    def home2(t, c):
+        a, b = CH * c, CH * c + CH
+        p = A("ps", 0, CH)
+        if t + 1 < NT:
+            copy(A("ls%d" % (t + 1), a, b), p)
+            send("li%d" % (t + 1), "ls%d" % (t + 1), a, b, "la%d%d" % (t + 1, c), me + 2 + t)
+            if t == 0:
+                copy(A("ot", 1024 + a, 1024 + b), p)
+        else:
+            act(A("yos", a, b), p, ACTF.Copy)
+        copy(A("kint", 8 * c, 8 * c + 8), A("nm%d" % t, 16 * c, 16 * c + 8))
+
+    def ext2(t):
+        p = A("pu", 0, G)
+        if t == 0:
+            copy(A("pt", 1024, 1536), p)
+        elif t == 1:
+            copy(A("ot", 1536, 2048), p)
+        else:
+            act(A("yps"), p, ACTF.Copy)
+            dma("y", "o_p", T.yp[:], T.yps[:], reads=[A("yps")])
+
+    def kand(t):
+        ts(A("kand"), A("kint"), 15, ALU.bitwise_and)
+        copy(A("kf"), A("kand"))
+
+    def verd1(t):
+        for k in range(16):
+            mm(A("pd1", k, 512, 16, p=8), A("ib", k, 128, 16), A("kf"), inc=k == 15)
+
+    def verd2(t):
+        act(A("yks", t * G, t * G + G, p=8), A("pd1", 0, 512, p=8), ACTF.Copy)
+        dma("y", "o_k%d" % t, T.yk[:, t * G:t * G + G], T.yks[0:8, t * G:t * G + G], reads=[A("yks", t * G, t * G + G)])
+
+    iota(A("pint", 0, 1), [[1, 1]], 0, 1)
+    iota(A("xint"), [[1, G]], 0, 0)
+    X, X144 = A("xx", 0, 128), A("xx", 0, 144)
+    ts(A("pint", 1, 2), A("pint", 0, 1), 15, ALU.bitwise_and)
+    copy(cp, A("pint", 0, 1))
+    copy(ck, A("pint", 1, 2))
+    tt(cg16, cp, ck, ALU.subtract)
+    ts(c37, ck, 37.0, ALU.mult)
+    ts(ct, cp, 0.0, ALU.is_equal, 32.0, ALU.mult)
+    ts(cg, cg16, 1.0 / 16, ALU.mult)
+    ts(cz15, cg16, 15.0, ALU.add)
+    ts(ct, ct, 32800.0, ALU.add)
+    copy(A("xx"), A("xint"))
+    send("zi0", "zst", 0, G, "za0", me + 1)
+    ts(A("xgi"), A("xint", 0, 128), 4, ALU.arith_shift_right)
+    ts(A("one"), A("xx"), 0.0, ALU.mult, 1.0, ALU.add)
+    copy(A("xg"), A("xgi"))
+    ts(A("kc"), X, 0.0, ALU.mult, ct, ALU.add)
+    ts(A("i4"), X, cp, ALU.is_equal, -4096.0, ALU.mult)
+    ts(A("ib"), X, cp, ALU.is_equal)
+    copy(A("mvu"), A("mvs"))
+    ts(A("nib"), X, cp, ALU.is_equal, -1.0, ALU.mult)
+    ts(A("zb_"), X144, cz15, ALU.is_equal)
+    ts(A("zh_"), X144, cz15, ALU.is_equal)
+    ts(A("bb"), A("xg"), cg, ALU.is_equal)
+    ts(A("tr2"), X, cp, ALU.is_gt)
+    ts(A("ih"), X, cp, ALU.is_equal)
+    tt(A("tr2"), A("tr2"), A("bb"), ALU.mult)
+    gather_v(A("ls0", 0, CH), A("pt", 0, 1024), A("mvu", 0, CH // 16))
+    send("li0", "ls0", 0, CH, "la0", me + 1)
+    gather_v(A("ls0", CH, G), A("pt", 0, 1024), A("mvu", CH // 16, 32))
+    send("li0", "ls0", CH, G, "lb0", me + 1)
+    copy(cw, A("wti", 0, 1))
+    ts(ck16, ck, 16.0, ALU.mult)
+    ts(A("bw"), A("xg"), cg, ALU.is_equal, cw, ALU.mult)
+    tt(A("tri"), A("ib"), A("tr2"), ALU.subtract)
+    fill(A("mhi"), 256.0)
+    fill(A("mlo"), 0.0)
+    fill(A("mhi", 0, 16 * CH, 16), 0.0)
+    fill(A("mlo", 0, 16 * CH, 16), 256.0)
+    ts(A("ani", 2, 3), A("pint", 0, 1), 3, ALU.bitwise_and)
+    ts(ct, ck, 15.0, ALU.is_equal, -100.0, ALU.mult)
+    ts(cthr, A("ani", 2, 3), float(min(QA)), ALU.is_ge, -7.0, ALU.mult)
+    ts(A("cst", 8, 16), A("xx", 0, 8), 0.0, ALU.mult)
+    tt(cthr, cthr, ct, ALU.add)
+    ts(A("cst", 0, 8), A("xx", 0, 8), 256.0, ALU.mult, ck16, ALU.add)
+    ts(cthr, cthr, 9.0, ALU.add)
+    addr(0, 0, CH)
+    afin(0, 0, CH)
+    mirror(0)
+    gath(0, 0, [s for s in range(4) if s not in DG])
+    gath(0, 0, DG, "v")
+    addr(0, CH, G)
+    afin(0, CH, G)
+    gath(0, 1, range(4))
+
+    def consts2():
+        ts(cj0, ck, 0.0, ALU.is_equal)
+        ts(cj1, ck, 1.0, ALU.is_equal)
+        ts(cnl, ck, 15.0, ALU.is_lt)
+        ts(cshp, cp, 1.0, ALU.add)
+        ts(c8k, ck, 8.0, ALU.mult)
+        ts(ct, ck, 15.0, ALU.is_equal, 1.0 / 4096, ALU.mult)
+        ts(A("it2"), A("xx"), cj0, ALU.mult, cj1, ALU.add)
+        for t in range(NT):
+            ts(cv[t], cj1, 1024.0 + 512 * t, ALU.mult)
+        ts(A("sh"), X, cshp, ALU.is_equal, cnl, ALU.mult)
+        for t in range(NT):
+            tt(cv[t], cv[t], cj0, ALU.add)
+        ts(A("zw_"), X144, cz15, ALU.is_equal, cw, ALU.mult)
+        ts(A("hib"), X, cp, ALU.is_equal, 0.5, ALU.mult)
+        for t in range(NT):
+            ts(A("nn%d" % t), X, cg16, ALU.is_equal, cv[t], ALU.mult)
+        ts(A("c8"), A("xx", 0, 32), 128.0, ALU.mult, c8k, ALU.add)
+        ts(A("a15"), X, 0.0, ALU.mult, ct, ALU.add)
+
+    for t in range(NT):
+        last = t + 1 == NT
+        if t:
+            afin(t, 0, CH)
+            gath(t, 0, [s for s in range(4) if s not in DG])
+            gath(t, 0, DG, "v")
+            afin(t, CH, 2 * CH)
+            gath(t, 1, (0, 1))
+            if t > 1:
+                verd2(t - 2)
+            home2(t - 1, 2)
+        for c in range(NC):
+            n = c + 1 if c + 1 < NC else None
+            j = None
+            if t and c < 2:
+                j = (t, CH * (c + 2), CH * (c + 3))
+            elif c == 3 and not last:
+                j = (t + 1, 0, CH)
+            if c == 0:
+                zx(t, c)
+                diff(t, c)
+            else:
+                cmps(t, c)
+            if j and c < 3:
+                addr1(*j)
+            cmpv(t, c)
+            if n and c:
+                gath(t, n, (0, 1))
+            if c:
+                lists2(t, c - 1)
+                pick1(t, c - 1)
+            else:
+                cmps(t, c)
+            scan(t, c, True)
+            count(t, c)
+            if c:
+                pick2(t, c - 1)
+            if c >= 2:
+                home2(t, c - 2)
+            if j and c < 3:
+                addr2(*j)
+            if t == 0 and c == 0:
+                consts2()
+            if t and c == 0:
+                home1(t - 1, 3)
+            hits(t, c)
+            if c == 1 and not last:
+                place1(t)
+            if c == 2:
+                shift(t, "ls%d" % t, 0, G, "pu")
+            if n and (c or t):
+                gath(t, n, (2, 3))
+            if c < 3:
+                scan(t, c, False)
+                if j:
+                    addr3(*j)
+                    afin(*j)
+            elif not last:
+                upd1(t, 0, 3 * CH)
+                upd2(t, 0, 3 * CH)
+                addr1(*j)
+                addr2(*j)
+            if t and c == 0:
+                home2(t - 1, 3)
+            if c + 1 < NC:
+                zx(t, c + 1)
+                diff(t, c + 1)
+            lists1(t, c)
+            if c == 3:
+                scan(t, c, False)
+                if not last:
+                    addr3(*j)
+                    scat(t, 0, 3 * CH)
+                    tally1(t)
+            if c == 1 and not last:
+                place2(t)
+                olds(t)
+            if c == 2:
+                ext2(t)
+            if 1 <= c < 3:
+                home1(t, c - 1)
+            if t and c == 1:
+                kand(t - 1)
+        if not last:
+            addr1(t + 1, CH, 2 * CH)
+        lists2(t, 3)
+        pick1(t, 3)
+        if not last:
+            mirror(t)
+            addr2(t + 1, CH, 2 * CH)
+        pick2(t, 3)
+        if not last:
+            upd1(t, 3 * CH, G)
+            tally2(t)
+            upd2(t, 3 * CH, G)
+            addr3(t + 1, CH, 2 * CH)
+            scat(t, 3 * CH, G)
+        home1(t, 2)
+        if t:
+            verd1(t - 1)
+    home2(2, 2)
+    verd2(1)
+    dma("y", "o_o0", T.yo[:, 0:3 * CH], T.yos[:, 0:3 * CH], reads=[A("yos", 0, 3 * CH)])
+    dma("y", "o_z0", T.yz[:, 0:3 * CH], T.zi3[:, 0:3 * CH], reads=[A("zi3", 0, 3 * CH)])
+    home1(2, 3)
+    home2(2, 3)
+    dma("s", "o_o1", T.yo[:, 3 * CH:G], T.yos[:, 3 * CH:G], reads=[A("yos", 3 * CH, G)])
+    kand(2)
+    verd1(2)
+    verd2(2)
+    dma("y", "o_z1", T.yz[:, 3 * CH:G], T.zi3[:, 3 * CH:G], reads=[A("zi3", 3 * CH, G)])
+    for s in OUTS + ["loc", "qv", "qs", "qp", "qg"]:
+        if cnt.get(s, 0) > known["g"].get(s, 0):
+            g.wait_ge(T.sem[s], cnt[s])

@@ -2,8 +2,8 @@ from concourse.mybir import AluOpType as ALU, AxisListType, ActivationFunctionTy
 
 NT, G, NC, CH = 3, 512, 4, 128
 RW = 4096 + 816
-QA = (3,)
 DG = (2, 3)
+BIG = 8388608.0
 EN = 8
 
 SCRATCH = {
@@ -15,6 +15,7 @@ SCRATCH = {
     "qf": ("sbuf", [128, G], "float16"), "xi": ("sbuf", [128, G], "int32"), "ai": ("sbuf", [128, G], "int32"),
     "hit": ("sbuf", [128, G], "bfloat16"), "oh": ("sbuf", [128, 2 * G], "float16"),
     "hp": ("sbuf", [128, G], "bfloat16"), "sm": ("sbuf", [128, G], "float16"), "z16": ("sbuf", [128, G], "float16"),
+    "lp": ("sbuf", [128, G], "bfloat16"), "big": ("sbuf", [128, G], "float32"), "nwb": ("sbuf", [128, G], "bfloat16"), "kq": ("sbuf", [128, 128], "float16"),
     "old": ("sbuf", [128, G], "bfloat16"), "nw": ("sbuf", [128, G], "int32"), "res": ("sbuf", [128, G], "float16"),
     "pli": ("sbuf", [128, 32], "int32"), "plm": ("sbuf", [128, 32], "int32"), "plu": ("sbuf", [128, 32], "uint16"),
     "kint": ("sbuf", [128, 32], "int32"), "kand": ("sbuf", [128, 32], "int32"), "kf": ("sbuf", [128, 32], "bfloat16"),
@@ -24,7 +25,7 @@ SCRATCH = {
     "pint": ("sbuf", [128, 8], "int32"), "col": ("sbuf", [128, 32], "float32"),
     "zb_": ("sbuf", [128, 144], "bfloat16"), "zh_": ("sbuf", [128, 144], "float16"), "zw_": ("sbuf", [128, 144], "bfloat16"),
     "bw": ("sbuf", [128, 128], "bfloat16"), "bb": ("sbuf", [128, 128], "bfloat16"), "ib": ("sbuf", [128, 128], "bfloat16"),
-    "nib": ("sbuf", [128, 128], "bfloat16"), "hib": ("sbuf", [128, 128], "bfloat16"), "ih": ("sbuf", [128, 128], "float16"),
+    "hib": ("sbuf", [128, 128], "bfloat16"), "ih": ("sbuf", [128, 128], "float16"),
     "i4": ("sbuf", [128, 128], "float16"), "sh": ("sbuf", [128, 128], "float16"), "tri": ("sbuf", [128, 128], "bfloat16"), "tr2": ("sbuf", [128, 128], "bfloat16"),
     "kc": ("sbuf", [128, 128], "float16"), "one": ("sbuf", [128, G], "float16"), "it2": ("sbuf", [128, G], "float16"),
     "a15": ("sbuf", [128, 128], "float32"), "cst": ("sbuf", [128, 16], "float16"), "c8": ("sbuf", [128, 32], "int32"),
@@ -45,7 +46,7 @@ for _b in BANKS:
 
 LDS = ["ld_mv", "ld_wt", "ld_z", "ld_p", "ld_o", "ld_r"]
 OUTS = ["o_p", "o_o0", "o_o1", "o_z0", "o_z1", "o_k0", "o_k1", "o_k2"]
-SEMAPHORES = ["qv", "qs", "qp", "qg", "loc", "za0", "la0", "lb0"] + LDS + OUTS
+SEMAPHORES = ["qv", "qs", "qp", "qg", "loc", "za0", "la0", "lb0", "lc0"] + LDS + OUTS
 for _t in range(NT):
     for _c in range(NC):
         SEMAPHORES += ["nm%d%d" % (_t, _c), "za%d%d" % (_t + 1, _c)]
@@ -153,10 +154,11 @@ def rank_program(g, core, T, topo):
         run("v", lambda q: q.tensor_tensor(out[0], a[0], b[0], op), [a, b], [out])
 
     def act(out, in_, fn, acc=None, **kw):
-        if acc is None:
-            run("s", lambda q: q.activation(out[0], in_[0], fn, **kw), [in_], [out])
-        else:
-            run("s", lambda q: q.activation(out[0], in_[0], fn, accum_out=acc[0], **kw), [in_], [out, acc])
+        rd = [in_] + [x for x in kw.values() if isinstance(x, tuple)]
+        kw = {n: x[0] if isinstance(x, tuple) else x for n, x in kw.items()}
+        if acc is not None:
+            kw["accum_out"] = acc[0]
+        run("s", lambda q: q.activation(out[0], in_[0], fn, **kw), rd, [out] if acc is None else [out, acc])
 
     def gather_v(out, win, off):
         run("v", lambda q: q.tensor_copy(out[0], win[0].indirect(off[0])), [win, off], [out])
@@ -172,7 +174,8 @@ def rank_program(g, core, T, topo):
 
     arrives("zi0", 0, G, "za0")
     arrives("li0", 0, CH, "la0")
-    arrives("li0", CH, G, "lb0")
+    arrives("li0", CH, 2 * CH, "lb0")
+    arrives("li0", 2 * CH, G, "lc0")
     for t in range(NT):
         for c in range(NC):
             arrives("nm%d" % t, 16 * c, 16 * c + 16, "nm%d%d" % (t, c))
@@ -226,26 +229,12 @@ def rank_program(g, core, T, topo):
         for e in range(4):
             mm(A("pz", e, 512, 4), A("ib"), A("zi%d" % t, CH * c, CH * c + CH), inc=e == 3)
 
-    def cmpv(t, c):
-        for q in range(4):
-            if q not in QA:
-                tt(A("bt", *blk(c, q)), A("yy", 2048 * c + q, 2048 * c + 2048, 4), A("pz"), ALU.is_gt)
-
-    def bank(c, q):
-        return "pd%d" % ((c * len(QA) + QA.index(q)) % 2)
-
-    def diff(t, c):
-        for q in QA:
-            mm(A(bank(c, q)), A("ib"), A("yy", 2048 * c + q, 2048 * c + 2048, 4), True, False)
-            for e in range(4):
-                mm(A(bank(c, q), e, 512, 4), A("nib"), A("zi%d" % t, CH * c, CH * c + CH), False, e == 3)
-
-    def cmps(t, c):
-        for q in QA:
-            act(A("bt", *blk(c, q)), A(bank(c, q)), ACTF.Sign, bias=-0.5)
+    def cmpv(t, c, qs):
+        for q in qs:
+            tt(A("bt", *blk(c, q)), A("yy", 2048 * c + q, 2048 * c + 2048, 4), A("pz"), ALU.is_gt)
 
     def count(t, c):
-        ks = [(q, m) for q in [q for q in range(4) if q not in QA] + list(QA) for m in range(4)]
+        ks = [(q, m) for q in range(4) for m in range(4)]
         for n, (q, m) in enumerate(ks):
             k = 4 * m + q
             lo, hi = blk(c, q)
@@ -261,11 +250,12 @@ def rank_program(g, core, T, topo):
     def hits(t, c):
         h = A("hit", CH * c, CH * c + CH)
         ts(h, A("pc", 0, CH), cthr, ALU.is_ge)
+        mm(A("pd0", 0, CH), A("tri"), h)
         mm(A("pf", 0, CH), A("tri"), h)
+        act(A("pr", 0, CH), A("pd0", 0, CH), ACTF.Relu, acc=A("acc", 4 * t + c, 4 * t + c + 1), scale=4096.0)
 
     def lists1(t, c):
         o = 2 * CH * c
-        act(A("pr", 0, CH), A("pf", 0, CH), ACTF.Relu, acc=A("acc", 4 * t + c, 4 * t + c + 1), scale=4096.0)
         ts(A("oh", o, o + CH), A("pf", 0, CH), 0.0, ALU.max, ck, ALU.mult)
         tt(A("oh", o + CH, o + 2 * CH), A("li%d" % t, CH * c, CH * c + CH), A("pr", 0, CH), ALU.min)
         pl = A("pf", 256, 272)
@@ -280,6 +270,25 @@ def rank_program(g, core, T, topo):
     def pick1(t, c):
         a, b = CH * c, CH * c + CH
         gather_s(A("hp", a, b), A("hi", 16 * a, 16 * b), A("sb%d" % t, 16 * c, 16 * c + 8))
+        if c < 3:
+            gather_s(A("lp", a, b), A("lo", 16 * a, 16 * b), A("sb%d" % t, 16 * c, 16 * c + 8))
+
+    def send_z(t, c):
+        send("zi%d" % (t + 1), "zo%d" % t, CH * c, CH * c + CH, "za%d%d" % (t + 1, c), me + 1 if t + 1 < NT else me - 1 - t)
+
+    def half(p, a, b, lo, hi):
+        mm(p, A("kq"), A("one", lo, hi), True, False)
+        mm(p, A("hib"), A(a, lo, hi), False, False)
+        mm(p, A("hib"), A(b, lo, hi), False, True)
+
+    def whole(out, p, lo, hi):
+        act(A("big", lo, hi), p, ACTF.Copy, bias=BIG)
+        act(A(out, lo, hi), A("big", lo, hi), ACTF.Copy, bias=-BIG)
+
+    def pick3(t, c):
+        half(A("pr", CH, 2 * CH), "hp", "lp", CH * c, CH * c + CH)
+        whole("zo%d" % t, A("pr", CH, 2 * CH), CH * c, CH * c + CH)
+        send_z(t, c)
 
     def pick2(t, c):
         a, b = CH * c, CH * c + CH
@@ -287,7 +296,7 @@ def rank_program(g, core, T, topo):
         run("v", lambda q: q.tensor_tensor(s[0], w[0].indirect(off[0]), h[0], ALU.add), [w, off, h], [s])
         ts(A("z16", a, b), s, 0.5, ALU.mult, 1024.75, ALU.add)
         ts(A("zo%d" % t, a, b), A("z16", a, b), -1025.0, ALU.add)
-        send("zi%d" % (t + 1), "zo%d" % t, a, b, "za%d%d" % (t + 1, c), me + 1 if t + 1 < NT else me - 1 - t)
+        send_z(t, c)
 
     def place1(t):
         for k in range(16):
@@ -309,11 +318,16 @@ def rank_program(g, core, T, topo):
     def upd2(t, lo, hi):
         ts(A("nw", lo, hi), A("ps", CH, CH + hi - lo), -0.25, ALU.add)
 
-    def scat(t, lo, hi):
-        w, o, i = A("rw", 0, 4096), A("plu", lo // 16, hi // 16), A("nw", lo, hi)
+    def upd3(t, lo, hi):
+        p = A("ps", CH, CH + hi - lo)
+        half(p, "old", "zo%d" % t, lo, hi)
+        whole("nwb", p, lo, hi)
+
+    def scat(t, lo, hi, src):
+        w, o, i = A("rw", 0, 4096), A("plu", lo // 16, hi // 16), A(src, lo, hi)
         run("v", lambda q: q.tensor_copy(w[0].indirect(o[0]), i[0]), [o, i], [w])
 
-    def mirror(t):
+    def mirror():
         copy(A("rw", 4096, RW), A("rw", 0, RW - 4096))
 
     def tally1(t):
@@ -334,7 +348,6 @@ def rank_program(g, core, T, topo):
     def home1(t, c):
         a, b = CH * c, CH * c + CH
         gather_v(A("res", a, b), A(("ot", "pt", "ot")[t], 0, 1024 + 512 * t), A("nm%d" % t, 16 * c + 8, 16 * c + 16))
-        shift(t, "res", a, b)
 
     def home2(t, c):
         a, b = CH * c, CH * c + CH
@@ -391,7 +404,7 @@ def rank_program(g, core, T, topo):
     ts(A("i4"), X, cp, ALU.is_equal, -4096.0, ALU.mult)
     ts(A("ib"), X, cp, ALU.is_equal)
     copy(A("mvu"), A("mvs"))
-    ts(A("nib"), X, cp, ALU.is_equal, -1.0, ALU.mult)
+    ts(A("kq"), X, 0.0, ALU.mult, -2.0 ** -9, ALU.add)
     ts(A("zb_"), X144, cz15, ALU.is_equal)
     ts(A("zh_"), X144, cz15, ALU.is_equal)
     ts(A("bb"), A("xg"), cg, ALU.is_equal)
@@ -401,50 +414,48 @@ def rank_program(g, core, T, topo):
     gather_v(A("ls0", 0, CH), A("pt", 0, 1024), A("mvu", 0, CH // 16))
     send("li0", "ls0", 0, CH, "la0", me + 1)
     gather_v(A("ls0", CH, G), A("pt", 0, 1024), A("mvu", CH // 16, 32))
-    send("li0", "ls0", CH, G, "lb0", me + 1)
+    send("li0", "ls0", CH, 2 * CH, "lb0", me + 1)
+    send("li0", "ls0", 2 * CH, G, "lc0", me + 1)
     copy(cw, A("wti", 0, 1))
     ts(ck16, ck, 16.0, ALU.mult)
     ts(A("bw"), A("xg"), cg, ALU.is_equal, cw, ALU.mult)
     tt(A("tri"), A("ib"), A("tr2"), ALU.subtract)
-    fill(A("mhi"), 256.0)
-    fill(A("mlo"), 0.0)
-    fill(A("mhi", 0, 16 * CH, 16), 0.0)
-    fill(A("mlo", 0, 16 * CH, 16), 256.0)
-    ts(A("ani", 2, 3), A("pint", 0, 1), 3, ALU.bitwise_and)
-    ts(ct, ck, 15.0, ALU.is_equal, -100.0, ALU.mult)
-    ts(cthr, A("ani", 2, 3), float(min(QA)), ALU.is_ge, -7.0, ALU.mult)
+    ts(ct, ck, 15.0, ALU.is_equal, 1.0 / 4096, ALU.mult)
+    act(A("hib"), A("ib"), ACTF.Copy, scale=0.5)
+    act(A("zw_"), A("zb_"), ACTF.Copy, scale=cw)
+    act(A("a15"), X, ACTF.Identity, scale=0.0, bias=ct)
+    for i in range(0, 16 * CH, G):
+        act(A("mhi", i, i + G), A("xx"), ACTF.Copy, scale=0.0, bias=256.0)
+        act(A("mlo", i, i + G), A("xx"), ACTF.Copy, scale=0.0)
+    act(A("mhi", 0, 16 * CH, 16), X, ACTF.Copy, scale=0.0)
+    act(A("mlo", 0, 16 * CH, 16), X, ACTF.Copy, scale=0.0, bias=256.0)
+    ts(cj0, ck, 0.0, ALU.is_equal)
+    ts(cj1, ck, 1.0, ALU.is_equal)
+    ts(cnl, ck, 15.0, ALU.is_lt)
+    ts(cshp, cp, 1.0, ALU.add)
+    ts(c8k, ck, 8.0, ALU.mult)
+    ts(A("it2"), A("xx"), cj0, ALU.mult, cj1, ALU.add)
+    for t in range(NT):
+        ts(cv[t], cj1, 1024.0 + 512 * t, ALU.mult)
+    ts(A("sh"), X, cshp, ALU.is_equal, cnl, ALU.mult)
+    for t in range(NT):
+        tt(cv[t], cv[t], cj0, ALU.add)
+    for t in range(NT):
+        ts(A("nn%d" % t), X, cg16, ALU.is_equal, cv[t], ALU.mult)
+    ts(A("c8"), A("xx", 0, 32), 128.0, ALU.mult, c8k, ALU.add)
+    ts(cthr, ck, 15.0, ALU.is_equal, -100.0, ALU.mult)
     ts(A("cst", 8, 16), A("xx", 0, 8), 0.0, ALU.mult)
-    tt(cthr, cthr, ct, ALU.add)
-    ts(A("cst", 0, 8), A("xx", 0, 8), 256.0, ALU.mult, ck16, ALU.add)
     ts(cthr, cthr, 9.0, ALU.add)
+    ts(A("cst", 0, 8), A("xx", 0, 8), 256.0, ALU.mult, ck16, ALU.add)
     addr(0, 0, CH)
     afin(0, 0, CH)
-    mirror(0)
+    mirror()
     gath(0, 0, [s for s in range(4) if s not in DG])
     gath(0, 0, DG, "v")
-    addr(0, CH, G)
-    afin(0, CH, G)
-    gath(0, 1, range(4))
-
-    def consts2():
-        ts(cj0, ck, 0.0, ALU.is_equal)
-        ts(cj1, ck, 1.0, ALU.is_equal)
-        ts(cnl, ck, 15.0, ALU.is_lt)
-        ts(cshp, cp, 1.0, ALU.add)
-        ts(c8k, ck, 8.0, ALU.mult)
-        ts(ct, ck, 15.0, ALU.is_equal, 1.0 / 4096, ALU.mult)
-        ts(A("it2"), A("xx"), cj0, ALU.mult, cj1, ALU.add)
-        for t in range(NT):
-            ts(cv[t], cj1, 1024.0 + 512 * t, ALU.mult)
-        ts(A("sh"), X, cshp, ALU.is_equal, cnl, ALU.mult)
-        for t in range(NT):
-            tt(cv[t], cv[t], cj0, ALU.add)
-        ts(A("zw_"), X144, cz15, ALU.is_equal, cw, ALU.mult)
-        ts(A("hib"), X, cp, ALU.is_equal, 0.5, ALU.mult)
-        for t in range(NT):
-            ts(A("nn%d" % t), X, cg16, ALU.is_equal, cv[t], ALU.mult)
-        ts(A("c8"), A("xx", 0, 32), 128.0, ALU.mult, c8k, ALU.add)
-        ts(A("a15"), X, 0.0, ALU.mult, ct, ALU.add)
+    addr(0, CH, 2 * CH)
+    afin(0, CH, 2 * CH)
+    gath(0, 1, (0, 1))
+    zx(0, 0)
 
     for t in range(NT):
         last = t + 1 == NT
@@ -452,105 +463,113 @@ def rank_program(g, core, T, topo):
             afin(t, 0, CH)
             gath(t, 0, [s for s in range(4) if s not in DG])
             gath(t, 0, DG, "v")
+            zx(t, 0)
+            addr3(t, CH, 2 * CH)
             afin(t, CH, 2 * CH)
             gath(t, 1, (0, 1))
+            home1(t - 1, 2)
+            shift(t - 1, "res", 2 * CH, 3 * CH)
             if t > 1:
+                verd1(t - 2)
                 verd2(t - 2)
-            home2(t - 1, 2)
         for c in range(NC):
             n = c + 1 if c + 1 < NC else None
             j = None
             if t and c < 2:
                 j = (t, CH * (c + 2), CH * (c + 3))
+            elif c == 0:
+                j = (0, 2 * CH, G)
             elif c == 3 and not last:
                 j = (t + 1, 0, CH)
-            if c == 0:
-                zx(t, c)
-                diff(t, c)
-            else:
-                cmps(t, c)
             if j and c < 3:
                 addr1(*j)
-            cmpv(t, c)
+            cmpv(t, c, (0, 1))
+            if t and c == 0:
+                home2(t - 1, 2)
             if n and c:
-                gath(t, n, (0, 1))
+                gath(t, n, (0,))
             if c:
                 lists2(t, c - 1)
                 pick1(t, c - 1)
-            else:
-                cmps(t, c)
+                if n:
+                    gath(t, n, (1,))
+            cmpv(t, c, (2, 3))
             scan(t, c, True)
             count(t, c)
             if c:
-                pick2(t, c - 1)
+                pick3(t, c - 1)
             if c >= 2:
-                home2(t, c - 2)
+                shift(t, "res", CH * (c - 2), CH * (c - 1))
             if j and c < 3:
                 addr2(*j)
-            if t == 0 and c == 0:
-                consts2()
             if t and c == 0:
                 home1(t - 1, 3)
+                shift(t - 1, "res", 3 * CH, G)
             hits(t, c)
             if c == 1 and not last:
                 place1(t)
             if c == 2:
                 shift(t, "ls%d" % t, 0, G, "pu")
-            if n and (c or t):
+            if n:
                 gath(t, n, (2, 3))
+            if c == 2 and not last:
+                olds(t)
+            if c == 3:
+                home2(t, 1)
             if c < 3:
                 scan(t, c, False)
-                if j:
+                if c == 2:
+                    home2(t, 0)
+                if j and c:
                     addr3(*j)
                     afin(*j)
             elif not last:
-                upd1(t, 0, 3 * CH)
-                upd2(t, 0, 3 * CH)
                 addr1(*j)
                 addr2(*j)
+                upd3(t, 0, 3 * CH)
             if t and c == 0:
                 home2(t - 1, 3)
             if c + 1 < NC:
                 zx(t, c + 1)
-                diff(t, c + 1)
             lists1(t, c)
+            if j and c == 0:
+                addr3(*j)
+                afin(*j)
             if c == 3:
                 scan(t, c, False)
                 if not last:
                     addr3(*j)
-                    scat(t, 0, 3 * CH)
-                    tally1(t)
             if c == 1 and not last:
                 place2(t)
-                olds(t)
             if c == 2:
                 ext2(t)
             if 1 <= c < 3:
                 home1(t, c - 1)
             if t and c == 1:
                 kand(t - 1)
-        if not last:
-            addr1(t + 1, CH, 2 * CH)
         lists2(t, 3)
         pick1(t, 3)
         if not last:
-            mirror(t)
+            addr1(t + 1, CH, 2 * CH)
+            scat(t, 0, 3 * CH, "nwb")
+            tally1(t)
+            act(A("rw", 4096, RW), A("rw", 0, RW - 4096), ACTF.Copy)
             addr2(t + 1, CH, 2 * CH)
         pick2(t, 3)
         if not last:
             upd1(t, 3 * CH, G)
             tally2(t)
             upd2(t, 3 * CH, G)
-            addr3(t + 1, CH, 2 * CH)
-            scat(t, 3 * CH, G)
-        home1(t, 2)
-        if t:
-            verd1(t - 1)
+            scat(t, 3 * CH, G, "nw")
+    home1(2, 2)
+    shift(2, "res", 2 * CH, 3 * CH)
+    verd1(1)
     home2(2, 2)
     verd2(1)
     dma("y", "o_o0", T.yo[:, 0:3 * CH], T.yos[:, 0:3 * CH], reads=[A("yos", 0, 3 * CH)])
     dma("y", "o_z0", T.yz[:, 0:3 * CH], T.zi3[:, 0:3 * CH], reads=[A("zi3", 0, 3 * CH)])
     home1(2, 3)
+    shift(2, "res", 3 * CH, G)
     home2(2, 3)
     dma("s", "o_o1", T.yo[:, 3 * CH:G], T.yos[:, 3 * CH:G], reads=[A("yos", 3 * CH, G)])
     kand(2)

from concourse.mybir import AluOpType as ALU, AxisListType, ActivationFunctionType as ACTF

NT, G, NC, CH = 3, 512, 4, 128
RW = 4096 + 816
DG = (2, 3)
BIG = 8388608.0
EN = 8

SCRATCH = {
    "rw": ("sbuf", [128, RW], "bfloat16"), "pt": ("sbuf", [128, 1536], "int32"), "ot": ("sbuf", [128, 2048], "int32"),
    "mvs": ("sbuf", [128, 32], "int32"), "mvu": ("sbuf", [128, 32], "uint16"),
    "wti": ("sbuf", [128, 8], "int32"), "zst": ("sbuf", [128, G], "bfloat16"),
    "yy": ("sbuf", [128, 16 * G], "bfloat16"), "hi": ("sbuf", [128, 16 * G], "bfloat16"), "lo": ("sbuf", [128, 16 * G], "bfloat16"),
    "bt": ("sbuf", [128, 16 * G], "bfloat16"), "mhi": ("sbuf", [128, 16 * CH], "bfloat16"), "mlo": ("sbuf", [128, 16 * CH], "bfloat16"),
    "qf": ("sbuf", [128, G], "float16"), "xi": ("sbuf", [128, G], "int32"), "ai": ("sbuf", [128, G], "int32"),
    "hit": ("sbuf", [128, G], "bfloat16"), "oh": ("sbuf", [128, 2 * G], "float16"),
    "hp": ("sbuf", [128, G], "bfloat16"), "sm": ("sbuf", [128, G], "float16"), "z16": ("sbuf", [128, G], "float16"),
    "lp": ("sbuf", [128, G], "bfloat16"), "big": ("sbuf", [128, G], "float32"), "nwb": ("sbuf", [128, G], "bfloat16"), "kq": ("sbuf", [128, 128], "float16"),
    "old": ("sbuf", [128, G], "bfloat16"), "nw": ("sbuf", [128, G], "int32"), "res": ("sbuf", [128, G], "float16"),
    "pli": ("sbuf", [128, 32], "int32"), "plm": ("sbuf", [128, 32], "int32"), "plu": ("sbuf", [128, 32], "uint16"),
    "kint": ("sbuf", [128, 32], "int32"), "kand": ("sbuf", [128, 32], "int32"), "kf": ("sbuf", [128, 32], "bfloat16"),
    "yps": ("sbuf", [128, G], "float32"), "yos": ("sbuf", [128, G], "float32"), "yks": ("sbuf", [128, NT * G], "float32"),
    "acc": ("sbuf", [128, 4 * NT], "float32"), "an": ("sbuf", [128, 4], "float32"), "ani": ("sbuf", [128, 8], "int32"),
    "xint": ("sbuf", [128, G], "int32"), "xgi": ("sbuf", [128, 128], "int32"), "xx": ("sbuf", [128, G], "float32"), "xg": ("sbuf", [128, 128], "float32"),
    "pint": ("sbuf", [128, 8], "int32"), "col": ("sbuf", [128, 32], "float32"),
    "zb_": ("sbuf", [128, 144], "bfloat16"), "zh_": ("sbuf", [128, 144], "float16"), "zw_": ("sbuf", [128, 144], "bfloat16"),
    "bw": ("sbuf", [128, 128], "bfloat16"), "bb": ("sbuf", [128, 128], "bfloat16"), "ib": ("sbuf", [128, 128], "bfloat16"),
    "hib": ("sbuf", [128, 128], "bfloat16"), "ih": ("sbuf", [128, 128], "float16"),
    "i4": ("sbuf", [128, 128], "float16"), "sh": ("sbuf", [128, 128], "float16"), "tri": ("sbuf", [128, 128], "bfloat16"), "tr2": ("sbuf", [128, 128], "bfloat16"),
    "kc": ("sbuf", [128, 128], "float16"), "one": ("sbuf", [128, G], "float16"), "it2": ("sbuf", [128, G], "float16"),
    "a15": ("sbuf", [128, 128], "float32"), "cst": ("sbuf", [128, 16], "float16"), "c8": ("sbuf", [128, 32], "int32"),
}
for _t in range(NT):
    SCRATCH["nn%d" % _t] = ("sbuf", [128, 128], "float16")
    SCRATCH["li%d" % _t] = ("sbuf", [128, G], "float16")
    SCRATCH["ls%d" % _t] = ("sbuf", [128, G], "float16")
    SCRATCH["of%d" % _t] = ("sbuf", [128, G], "uint16")
    SCRATCH["sb%d" % _t] = ("sbuf", [128, 16 * NC], "uint16")
    SCRATCH["nm%d" % _t] = ("sbuf", [128, 16 * NC], "uint16")
    SCRATCH["zo%d" % _t] = ("sbuf", [128, G], "bfloat16")
for _t in range(NT + 1):
    SCRATCH["zi%d" % _t] = ("sbuf", [128, G], "bfloat16")
BANKS = ("pz", "pd0", "pd1", "pc", "pf", "pr", "pu", "ps")
for _b in BANKS:
    SCRATCH[_b] = ("psum", [128, 512], "float32")

LDS = ["ld_mv", "ld_wt", "ld_z", "ld_p", "ld_o", "ld_r"]
OUTS = ["o_p", "o_o0", "o_o1", "o_z0", "o_z1", "o_k0", "o_k1", "o_k2"]
SEMAPHORES = ["qv", "qs", "qp", "qg", "loc", "za0", "la0", "lb0", "lc0"] + LDS + OUTS
for _t in range(NT):
    for _c in range(NC):
        SEMAPHORES += ["nm%d%d" % (_t, _c), "za%d%d" % (_t + 1, _c)]
        if _t:
            SEMAPHORES.append("la%d%d" % (_t, _c))


def rank_program(g, core, T, topo):
    me = T.rank_of(core)
    if me is None:
        return
    cores = list(T.cores)
    N = len(cores)
    Q = {"v": g.vector, "s": g.scalar, "p": g.tensor, "g": g, "y": g.sync}
    cnt, known, recs = {}, {e: {} for e in Q}, {}

    def need(e, tok):
        sem, val, vc = tok
        k = known[e]
        if k.get(sem, 0) >= val:
            return
        Q[e].wait_ge(T.sem[sem], val)
        k[sem] = val
        for s2, v2 in vc.items():
            if k.get(s2, 0) < v2:
                k[s2] = v2

    def deps(e, eng, reads, writes):
        for w, lst in ((0, reads), (1, writes)):
            for n, lo, hi in lst:
                for rec in recs.get(n, ()):
                    if n in BANKS:
                        hit = rec[3] != eng or (eng != "p" and (w or rec[2]))
                    else:
                        hit = rec[0] < hi and lo < rec[1] and (rec[2] or (w and rec[3] != eng))
                    if hit:
                        need(e, rec[4])

    def note(eng, tok, reads, writes):
        for w, lst in ((0, reads), (1, writes)):
            for n, lo, hi in lst:
                old = recs.get(n, [])
                if n in BANKS:
                    w0 = any(r[2] for r in old if r[3] == eng)
                    recs[n] = [(lo, hi, w or w0, eng, tok)]
                    continue
                if w:
                    old = [r for r in old if not (lo <= r[0] and r[1] <= hi)]
                else:
                    old = [r for r in old if not (r[3] == eng and not r[2] and lo <= r[0] and r[1] <= hi)]
                recs[n] = old + [(lo, hi, w, eng, tok)]

    def A(n, lo=0, hi=None, st=1, p=128):
        t = T[n]
        hi = t.shape[1] if hi is None else hi
        return (t[0:p, lo:hi:st], (n, lo, hi)) if st > 1 else (t[0:p, lo:hi], (n, lo, hi))

    def run(e, fn, reads, writes, inc=True):
        rd, wr = [r[1] for r in reads], [w[1] for w in writes]
        deps(e, e, rd, wr)
        ins = fn(Q[e])
        sem = "q" + e
        val = cnt.get(sem, 0) + 1
        if inc:
            ins.then_inc(T.sem[sem], 1)
            cnt[sem] = val
        note(e, (sem, val, dict(known[e])), rd, wr)

    def dma(e, sem, out, in_, reads=(), writes=()):
        rd, wr = [r[1] for r in reads], [w[1] for w in writes]
        deps(e, "d" + sem, rd, wr)
        Q[e].dma_start(out, in_).then_inc(T.sem[sem], 16)
        cnt[sem] = cnt.get(sem, 0) + 16
        note("d" + sem, (sem, cnt[sem], dict(known[e])), rd, wr)

    def arrives(buf, lo, hi, sem):
        recs.setdefault(buf, []).append((lo, hi, 1, "r", (sem, EN, {})))

    def send(buf, src, lo, hi, sem, to):
        dst = cores[to % N]
        deps("g", "r", [(src, lo, hi)], [])
        rid, pid, _ = topo.addr(dst)
        m = 0
        for x in topo.engines(core, dst)[:EN]:
            m |= 1 << x
        g.remote_dma(T[buf][:, lo:hi], T[src][:, lo:hi], T.sem[sem], T.sem["loc"], pid, rid, m)
        cnt["loc"] = cnt.get("loc", 0) + EN

    def mm(out, l, r, start=True, stop=True, inc=None):
        run("p", lambda q: q.matmul(out[0], l[0], r[0], start, stop), [l, r], [out], stop if inc is None else inc)

    def copy(out, in_):
        run("v", lambda q: q.tensor_copy(out[0], in_[0]), [in_], [out])

    def ts(out, in_, s1, op0, s2=None, op1=None):
        rd = [in_] + [s for s in (s1, s2) if isinstance(s, tuple)]
        a1 = s1[0] if isinstance(s1, tuple) else s1
        a2 = s2[0] if isinstance(s2, tuple) else s2
        if op1 is None:
            run("v", lambda q: q.tensor_scalar(out[0], in_[0], a1, None, op0), rd, [out])
        else:
            run("v", lambda q: q.tensor_scalar(out[0], in_[0], a1, a2, op0, op1), rd, [out])

    def tt(out, a, b, op):
        run("v", lambda q: q.tensor_tensor(out[0], a[0], b[0], op), [a, b], [out])

    def act(out, in_, fn, acc=None, **kw):
        rd = [in_] + [x for x in kw.values() if isinstance(x, tuple)]
        kw = {n: x[0] if isinstance(x, tuple) else x for n, x in kw.items()}
        if acc is not None:
            kw["accum_out"] = acc[0]
        run("s", lambda q: q.activation(out[0], in_[0], fn, **kw), rd, [out] if acc is None else [out, acc])

    def gather_v(out, win, off):
        run("v", lambda q: q.tensor_copy(out[0], win[0].indirect(off[0])), [win, off], [out])

    def gather_s(out, win, off):
        run("s", lambda q: q.activation(out[0], win[0].indirect(off[0]), ACTF.Copy), [win, off], [out])

    def fill(out, c):
        run("v", lambda q: q.memset(out[0], c), [], [out])

    def iota(out, pattern, base, cm):
        run("g", lambda q: q.iota(out[0], pattern, base, cm), [], [out])

    arrives("zi0", 0, G, "za0")
    arrives("li0", 0, CH, "la0")
    arrives("li0", CH, 2 * CH, "lb0")
    arrives("li0", 2 * CH, G, "lc0")
    for t in range(NT):
        for c in range(NC):
            arrives("nm%d" % t, 16 * c, 16 * c + 16, "nm%d%d" % (t, c))
            arrives("zi%d" % (t + 1), CH * c, CH * c + CH, "za%d%d" % (t + 1, c))
            if t:
                arrives("li%d" % t, CH * c, CH * c + CH, "la%d%d" % (t, c))

    dma("s", "ld_z", T.zst[:], T.z0[:], writes=[A("zst")])
    dma("y", "ld_mv", T.mvs[:], T.mv[:], writes=[A("mvs")])
    dma("y", "ld_p", T.pt[:, 0:1024], T.vp[:], writes=[A("pt", 0, 1024)])
    dma("s", "ld_wt", T.wti[:, 0:1], T.wt[:], writes=[A("wti", 0, 1)])
    dma("s", "ld_r", T.rw[:, 0:4096], T.strat[:], writes=[A("rw", 0, 4096)])
    dma("y", "ld_o", T.ot[:, 0:1024], T.vo[:], writes=[A("ot", 0, 1024)])

    C = lambda i: A("col", i, i + 1)
    cp, ck, cg16, cz15, c37, ck16, c8k, cj0, cj1, cnl, cshp, cthr, cw, cg, ct, cadd = [C(i) for i in range(16)]
    cv = [C(16 + i) for i in range(NT)]

    def addr1(t, lo, hi):
        mm(A("pu", 0, hi - lo), A("bw"), A("zi%d" % t, lo, hi))

    def addr2(t, lo, hi):
        n = hi - lo
        pu = A("pu", 0, n)
        ts(A("qf", lo, hi), pu, 1.0 / 4096, ALU.mult, 1025 - 2047.5 / 4096, ALU.add)
        mm(pu, A("kc"), A("one", 0, n), True, False)
        mm(pu, A("bw"), A("zi%d" % t, lo, hi), False, False)
        mm(pu, A("i4"), A("qf", lo, hi), False, True)

    def addr3(t, lo, hi):
        tt(A("xi", lo, hi), A("li%d" % t, lo, hi), A("pu", 0, hi - lo), ALU.mult)
        ts(A("ai", lo, hi), A("xi", lo, hi), 5, ALU.arith_shift_right, 4095, ALU.bitwise_and)

    def addr(t, lo, hi):
        addr1(t, lo, hi)
        addr2(t, lo, hi)
        addr3(t, lo, hi)

    def afin(t, lo, hi):
        ts(A("of%d" % t, lo, hi), A("ai", lo, hi), cadd if t else c37, ALU.add)

    def gath(t, c, pieces, e="s"):
        for s in pieces:
            i0 = CH * c + 32 * s
            (gather_s if e == "s" else gather_v)(A("yy", 16 * i0, 16 * i0 + 512), A("rw", 0, RW), A("of%d" % t, i0, i0 + 32))

    def blk(c, q):
        return (2048 * c + 512 * q, 2048 * c + 512 * q + 512)

    def zx(t, c):
        for e in range(4):
            mm(A("pz", e, 512, 4), A("ib"), A("zi%d" % t, CH * c, CH * c + CH), inc=e == 3)

    def cmpv(t, c, qs):
        for q in qs:
            tt(A("bt", *blk(c, q)), A("yy", 2048 * c + q, 2048 * c + 2048, 4), A("pz"), ALU.is_gt)

    def count(t, c):
        ks = [(q, m) for q in range(4) for m in range(4)]
        for n, (q, m) in enumerate(ks):
            k = 4 * m + q
            lo, hi = blk(c, q)
            mm(A("pc", 0, CH), A("zb_", 15 - k, 143 - k), A("bt", lo + m, hi, 4), n == 0, n == 15)

    def scan(t, c, hi):
        s = (2048 * c, 2048 * c + 2048)
        o, m = (A("hi", *s), A("mhi")) if hi else (A("lo", *s), A("mlo"))
        o0, o1 = (ALU.min, ALU.max) if hi else (ALU.max, ALU.min)
        y = A("yy", *s)
        run("v", lambda q: q.tensor_tensor_scan(o[0], m[0], y[0], 0.0, o0, o1), [m, y], [o])

    def hits(t, c):
        h = A("hit", CH * c, CH * c + CH)
        ts(h, A("pc", 0, CH), cthr, ALU.is_ge)
        mm(A("pd0", 0, CH), A("tri"), h)
        mm(A("pf", 0, CH), A("tri"), h)
        act(A("pr", 0, CH), A("pd0", 0, CH), ACTF.Relu, acc=A("acc", 4 * t + c, 4 * t + c + 1), scale=4096.0)

    def lists1(t, c):
        o = 2 * CH * c
        ts(A("oh", o, o + CH), A("pf", 0, CH), 0.0, ALU.max, ck, ALU.mult)
        tt(A("oh", o + CH, o + 2 * CH), A("li%d" % t, CH * c, CH * c + CH), A("pr", 0, CH), ALU.min)
        pl = A("pf", 256, 272)
        mm(pl, A("ih"), A("cst"), True, False)
        for k in range(16):
            mm(pl, A("zh_", 15 - k, 143 - k), A("oh", o + k, o + 2 * CH, 16), False, k == 15)

    def lists2(t, c):
        copy(A("sb%d" % t, 16 * c, 16 * c + 16), A("pf", 256, 272))
        send("nm%d" % t, "sb%d" % t, 16 * c, 16 * c + 16, "nm%d%d" % (t, c), me - 1 - t)

    def pick1(t, c):
        a, b = CH * c, CH * c + CH
        gather_s(A("hp", a, b), A("hi", 16 * a, 16 * b), A("sb%d" % t, 16 * c, 16 * c + 8))
        if c < 3:
            gather_s(A("lp", a, b), A("lo", 16 * a, 16 * b), A("sb%d" % t, 16 * c, 16 * c + 8))

    def send_z(t, c):
        send("zi%d" % (t + 1), "zo%d" % t, CH * c, CH * c + CH, "za%d%d" % (t + 1, c), me + 1 if t + 1 < NT else me - 1 - t)

    def half(p, a, b, lo, hi):
        mm(p, A("kq"), A("one", lo, hi), True, False)
        mm(p, A("hib"), A(a, lo, hi), False, False)
        mm(p, A("hib"), A(b, lo, hi), False, True)

    def whole(out, p, lo, hi):
        act(A("big", lo, hi), p, ACTF.Copy, bias=BIG)
        act(A(out, lo, hi), A("big", lo, hi), ACTF.Copy, bias=-BIG)

    def pick3(t, c):
        half(A("pr", CH, 2 * CH), "hp", "lp", CH * c, CH * c + CH)
        whole("zo%d" % t, A("pr", CH, 2 * CH), CH * c, CH * c + CH)
        send_z(t, c)

    def pick2(t, c):
        a, b = CH * c, CH * c + CH
        off, w, h, s = A("sb%d" % t, 16 * c, 16 * c + 8), A("lo", 16 * a, 16 * b), A("hp", a, b), A("sm", a, b)
        run("v", lambda q: q.tensor_tensor(s[0], w[0].indirect(off[0]), h[0], ALU.add), [w, off, h], [s])
        ts(A("z16", a, b), s, 0.5, ALU.mult, 1024.75, ALU.add)
        ts(A("zo%d" % t, a, b), A("z16", a, b), -1025.0, ALU.add)
        send_z(t, c)

    def place1(t):
        for k in range(16):
            mm(A("pr", 256, 288), A("zw_", 15 - k, 143 - k), A("zi%d" % t, k, G, 16), k == 0, k == 15)

    def place2(t):
        copy(A("pli"), A("pr", 256, 288))
        ts(A("plm"), A("pli"), 7, ALU.bitwise_and)
        tt(A("pli"), A("plm"), A("c8"), ALU.add)
        copy(A("plu"), A("pli"))

    def olds(t):
        gather_s(A("old"), A("rw", 0, 4096), A("plu"))

    def upd1(t, lo, hi):
        mm(A("ps", CH, CH + hi - lo), A("hib"), A("old", lo, hi), True, False)
        mm(A("ps", CH, CH + hi - lo), A("hib"), A("zo%d" % t, lo, hi), False, True)

    def upd2(t, lo, hi):
        ts(A("nw", lo, hi), A("ps", CH, CH + hi - lo), -0.25, ALU.add)

    def upd3(t, lo, hi):
        p = A("ps", CH, CH + hi - lo)
        half(p, "old", "zo%d" % t, lo, hi)
        whole("nwb", p, lo, hi)

    def scat(t, lo, hi, src):
        w, o, i = A("rw", 0, 4096), A("plu", lo // 16, hi // 16), A(src, lo, hi)
        run("v", lambda q: q.tensor_copy(w[0].indirect(o[0]), i[0]), [o, i], [w])

    def mirror():
        copy(A("rw", 4096, RW), A("rw", 0, RW - 4096))

    def tally1(t):
        mm(A("pr", 320, 324), A("a15"), A("acc", 4 * t, 4 * t + 4))

    def tally2(t):
        o, i = A("an", 0, 1), A("pr", 320, 324)
        run("v", lambda q: q.tensor_reduce(o[0], i[0], AxisListType.X, ALU.add, negate=True), [i], [o])
        copy(A("ani", 0, 1), o)
        ts(A("ani", 1, 2), A("ani", 0, 1), 255, ALU.bitwise_and)
        ts(cadd, A("ani", 1, 2), c37, ALU.add)

    def shift(t, src, lo, hi, b="ps"):
        p = A(b, 0, hi - lo)
        mm(p, A("sh"), A(src, lo, hi), True, False)
        mm(p, A("nn%d" % t), A("it2", lo, hi), False, True)

    def home1(t, c):
        a, b = CH * c, CH * c + CH
        gather_v(A("res", a, b), A(("ot", "pt", "ot")[t], 0, 1024 + 512 * t), A("nm%d" % t, 16 * c + 8, 16 * c + 16))

    def home2(t, c):
        a, b = CH * c, CH * c + CH
        p = A("ps", 0, CH)
        if t + 1 < NT:
            copy(A("ls%d" % (t + 1), a, b), p)
            send("li%d" % (t + 1), "ls%d" % (t + 1), a, b, "la%d%d" % (t + 1, c), me + 2 + t)
            if t == 0:
                copy(A("ot", 1024 + a, 1024 + b), p)
        else:
            act(A("yos", a, b), p, ACTF.Copy)
        copy(A("kint", 8 * c, 8 * c + 8), A("nm%d" % t, 16 * c, 16 * c + 8))

    def ext2(t):
        p = A("pu", 0, G)
        if t == 0:
            copy(A("pt", 1024, 1536), p)
        elif t == 1:
            copy(A("ot", 1536, 2048), p)
        else:
            act(A("yps"), p, ACTF.Copy)
            dma("y", "o_p", T.yp[:], T.yps[:], reads=[A("yps")])

    def kand(t):
        ts(A("kand"), A("kint"), 15, ALU.bitwise_and)
        copy(A("kf"), A("kand"))

    def verd1(t):
        for k in range(16):
            mm(A("pd1", k, 512, 16, p=8), A("ib", k, 128, 16), A("kf"), inc=k == 15)

    def verd2(t):
        act(A("yks", t * G, t * G + G, p=8), A("pd1", 0, 512, p=8), ACTF.Copy)
        dma("y", "o_k%d" % t, T.yk[:, t * G:t * G + G], T.yks[0:8, t * G:t * G + G], reads=[A("yks", t * G, t * G + G)])

    iota(A("pint", 0, 1), [[1, 1]], 0, 1)
    iota(A("xint"), [[1, G]], 0, 0)
    X, X144 = A("xx", 0, 128), A("xx", 0, 144)
    ts(A("pint", 1, 2), A("pint", 0, 1), 15, ALU.bitwise_and)
    copy(cp, A("pint", 0, 1))
    copy(ck, A("pint", 1, 2))
    tt(cg16, cp, ck, ALU.subtract)
    ts(c37, ck, 37.0, ALU.mult)
    ts(ct, cp, 0.0, ALU.is_equal, 32.0, ALU.mult)
    ts(cg, cg16, 1.0 / 16, ALU.mult)
    ts(cz15, cg16, 15.0, ALU.add)
    ts(ct, ct, 32800.0, ALU.add)
    copy(A("xx"), A("xint"))
    send("zi0", "zst", 0, G, "za0", me + 1)
    ts(A("xgi"), A("xint", 0, 128), 4, ALU.arith_shift_right)
    ts(A("one"), A("xx"), 0.0, ALU.mult, 1.0, ALU.add)
    copy(A("xg"), A("xgi"))
    ts(A("kc"), X, 0.0, ALU.mult, ct, ALU.add)
    ts(A("i4"), X, cp, ALU.is_equal, -4096.0, ALU.mult)
    ts(A("ib"), X, cp, ALU.is_equal)
    copy(A("mvu"), A("mvs"))
    ts(A("kq"), X, 0.0, ALU.mult, -2.0 ** -9, ALU.add)
    ts(A("zb_"), X144, cz15, ALU.is_equal)
    ts(A("zh_"), X144, cz15, ALU.is_equal)
    ts(A("bb"), A("xg"), cg, ALU.is_equal)
    ts(A("tr2"), X, cp, ALU.is_gt)
    ts(A("ih"), X, cp, ALU.is_equal)
    tt(A("tr2"), A("tr2"), A("bb"), ALU.mult)
    gather_v(A("ls0", 0, CH), A("pt", 0, 1024), A("mvu", 0, CH // 16))
    send("li0", "ls0", 0, CH, "la0", me + 1)
    gather_v(A("ls0", CH, G), A("pt", 0, 1024), A("mvu", CH // 16, 32))
    send("li0", "ls0", CH, 2 * CH, "lb0", me + 1)
    send("li0", "ls0", 2 * CH, G, "lc0", me + 1)
    copy(cw, A("wti", 0, 1))
    ts(ck16, ck, 16.0, ALU.mult)
    ts(A("bw"), A("xg"), cg, ALU.is_equal, cw, ALU.mult)
    tt(A("tri"), A("ib"), A("tr2"), ALU.subtract)
    ts(ct, ck, 15.0, ALU.is_equal, 1.0 / 4096, ALU.mult)
    act(A("hib"), A("ib"), ACTF.Copy, scale=0.5)
    act(A("zw_"), A("zb_"), ACTF.Copy, scale=cw)
    act(A("a15"), X, ACTF.Identity, scale=0.0, bias=ct)
    for i in range(0, 16 * CH, G):
        act(A("mhi", i, i + G), A("xx"), ACTF.Copy, scale=0.0, bias=256.0)
        act(A("mlo", i, i + G), A("xx"), ACTF.Copy, scale=0.0)
    act(A("mhi", 0, 16 * CH, 16), X, ACTF.Copy, scale=0.0)
    act(A("mlo", 0, 16 * CH, 16), X, ACTF.Copy, scale=0.0, bias=256.0)
    ts(cj0, ck, 0.0, ALU.is_equal)
    ts(cj1, ck, 1.0, ALU.is_equal)
    ts(cnl, ck, 15.0, ALU.is_lt)
    ts(cshp, cp, 1.0, ALU.add)
    ts(c8k, ck, 8.0, ALU.mult)
    ts(A("it2"), A("xx"), cj0, ALU.mult, cj1, ALU.add)
    for t in range(NT):
        ts(cv[t], cj1, 1024.0 + 512 * t, ALU.mult)
    ts(A("sh"), X, cshp, ALU.is_equal, cnl, ALU.mult)
    for t in range(NT):
        tt(cv[t], cv[t], cj0, ALU.add)
    for t in range(NT):
        ts(A("nn%d" % t), X, cg16, ALU.is_equal, cv[t], ALU.mult)
    ts(A("c8"), A("xx", 0, 32), 128.0, ALU.mult, c8k, ALU.add)
    ts(cthr, ck, 15.0, ALU.is_equal, -100.0, ALU.mult)
    ts(A("cst", 8, 16), A("xx", 0, 8), 0.0, ALU.mult)
    ts(cthr, cthr, 9.0, ALU.add)
    ts(A("cst", 0, 8), A("xx", 0, 8), 256.0, ALU.mult, ck16, ALU.add)
    addr(0, 0, CH)
    afin(0, 0, CH)
    mirror()
    gath(0, 0, [s for s in range(4) if s not in DG])
    gath(0, 0, DG, "v")
    addr(0, CH, 2 * CH)
    afin(0, CH, 2 * CH)
    gath(0, 1, (0, 1))
    zx(0, 0)

    for t in range(NT):
        last = t + 1 == NT
        if t:
            afin(t, 0, CH)
            gath(t, 0, [s for s in range(4) if s not in DG])
            gath(t, 0, DG, "v")
            zx(t, 0)
            addr3(t, CH, 2 * CH)
            afin(t, CH, 2 * CH)
            gath(t, 1, (0, 1))
            home1(t - 1, 2)
            shift(t - 1, "res", 2 * CH, 3 * CH)
            if t > 1:
                verd1(t - 2)
                verd2(t - 2)
        for c in range(NC):
            n = c + 1 if c + 1 < NC else None
            j = None
            if t and c < 2:
                j = (t, CH * (c + 2), CH * (c + 3))
            elif c == 0:
                j = (0, 2 * CH, G)
            elif c == 3 and not last:
                j = (t + 1, 0, CH)
            if j and c < 3:
                addr1(*j)
            cmpv(t, c, (0, 1))
            if t and c == 0:
                home2(t - 1, 2)
            if n and c:
                gath(t, n, (0,))
            if c:
                lists2(t, c - 1)
                pick1(t, c - 1)
                if n:
                    gath(t, n, (1,))
            cmpv(t, c, (2, 3))
            scan(t, c, True)
            count(t, c)
            if c:
                pick3(t, c - 1)
            if c >= 2:
                shift(t, "res", CH * (c - 2), CH * (c - 1))
            if j and c < 3:
                addr2(*j)
            if t and c == 0:
                home1(t - 1, 3)
                shift(t - 1, "res", 3 * CH, G)
            hits(t, c)
            if c == 1 and not last:
                place1(t)
            if c == 2:
                shift(t, "ls%d" % t, 0, G, "pu")
            if n:
                gath(t, n, (2, 3))
            if c == 2 and not last:
                olds(t)
            if c == 3:
                home2(t, 1)
            if c < 3:
                scan(t, c, False)
                if c == 2:
                    home2(t, 0)
                if j and c:
                    addr3(*j)
                    afin(*j)
            elif not last:
                addr1(*j)
                addr2(*j)
                upd3(t, 0, 3 * CH)
            if t and c == 0:
                home2(t - 1, 3)
            if c + 1 < NC:
                zx(t, c + 1)
            lists1(t, c)
            if j and c == 0:
                addr3(*j)
                afin(*j)
            if c == 3:
                scan(t, c, False)
                if not last:
                    addr3(*j)
            if c == 1 and not last:
                place2(t)
            if c == 2:
                ext2(t)
            if 1 <= c < 3:
                home1(t, c - 1)
            if t and c == 1:
                kand(t - 1)
        lists2(t, 3)
        pick1(t, 3)
        if not last:
            addr1(t + 1, CH, 2 * CH)
            scat(t, 0, 3 * CH, "nwb")
            tally1(t)
            act(A("rw", 4096, RW), A("rw", 0, RW - 4096), ACTF.Copy)
            addr2(t + 1, CH, 2 * CH)
        pick2(t, 3)
        if not last:
            upd1(t, 3 * CH, G)
            tally2(t)
            upd2(t, 3 * CH, G)
            scat(t, 3 * CH, G, "nw")
    home1(2, 2)
    shift(2, "res", 2 * CH, 3 * CH)
    verd1(1)
    home2(2, 2)
    verd2(1)
    dma("y", "o_o0", T.yo[:, 0:3 * CH], T.yos[:, 0:3 * CH], reads=[A("yos", 0, 3 * CH)])
    dma("y", "o_z0", T.yz[:, 0:3 * CH], T.zi3[:, 0:3 * CH], reads=[A("zi3", 0, 3 * CH)])
    home1(2, 3)
    shift(2, "res", 3 * CH, G)
    home2(2, 3)
    dma("s", "o_o1", T.yo[:, 3 * CH:G], T.yos[:, 3 * CH:G], reads=[A("yos", 3 * CH, G)])
    kand(2)
    verd1(2)
    verd2(2)
    dma("y", "o_z1", T.yz[:, 3 * CH:G], T.zi3[:, 3 * CH:G], reads=[A("zi3", 3 * CH, G)])
    for s in OUTS + ["loc", "qv", "qs", "qp", "qg"]:
        if cnt.get(s, 0) > known["g"].get(s, 0):
            g.wait_ge(T.sem[s], cnt[s])
